import numpy as np
import ml_dtypes


def mxq(x, axis, fmt="e4m3"):
    dtype, down = {"e4m3": (ml_dtypes.float8_e4m3fn, 7), "e5m2": (ml_dtypes.float8_e5m2, 14)}[fmt]
    v = np.moveaxis(np.asarray(x, np.float32).astype(ml_dtypes.bfloat16).astype(np.float64), axis, -1)
    blocks = v.reshape(v.shape[:-1] + (-1, 32))
    amax = np.abs(blocks).max(-1, keepdims=True)
    byte = np.maximum(np.where(amax > 0, np.frexp(amax)[1] - 1 + 127, 0) - down, 1)
    scale = np.exp2(byte - 127.0)
    codes = (blocks / scale).astype(np.float32).astype(dtype).astype(np.float64)
    return np.moveaxis((codes * scale).reshape(v.shape), -1, axis)


WIDE = False


def mx_kscale(k):
    if not WIDE:
        return np.ones(k)
    levels = np.array([10, -10, 5, -5, 0])
    if k % 512:
        return np.exp2(np.random.permutation(np.resize(levels, k // 32))).repeat(32)
    a = np.empty((k // 512, 16))
    for p in range(k // 512):
        a[p, :8] = np.random.permutation(np.resize(levels, 8))
        for g in range(8):
            far = levels[np.abs(levels - a[p, g]) >= 10]
            a[p, g + 8] = far[np.random.randint(len(far))]
    return np.exp2(a.ravel()).repeat(32)


def f64(x):
    return np.asarray(x).astype(np.float64)


def striped(idx):
    return np.tile(idx.reshape(-1, 16).T, (8, 1)).astype(np.uint16)


def unstriped(offs):
    return offs[:16].T.reshape(-1).astype(np.int64)


E2M1 = np.array([0.0, 0.5, 1.0, 1.5, 2.0, 3.0, 4.0, 6.0, -0.0, -0.5, -1.0, -1.5, -2.0, -3.0, -4.0, -6.0])


def pack_fp4(w):
    k, n = w.shape
    w = f64(np.asarray(w, np.float32).astype(ml_dtypes.bfloat16)).reshape(k // 32, 32, n)
    amax = np.abs(w).max(1)
    mant, ex = np.frexp(amax / 6.0)
    byte = np.clip(np.where(amax > 0, np.where(mant > 0.5, ex, ex - 1) + 127, 1), 1, 254)
    scaled = (w * np.exp2(127.0 - byte)[:, None, :]).reshape(k, n).astype(np.float32)
    c = np.ascontiguousarray(scaled.reshape(k // 512, 128, 4, n).transpose(0, 1, 3, 2)).astype(ml_dtypes.float4_e2m1fn).view(np.uint8) & 0xF
    words = (c[..., 0::2] | (c[..., 1::2] << 4)).reshape(k // 512, 128, 2 * n)
    return np.ascontiguousarray(words), np.ascontiguousarray(byte.astype(np.uint8).reshape(k // 512, 16, n))


def unpack_fp4(words, scales):
    g, _, n = scales.shape
    words = np.ascontiguousarray(words).reshape(g, 128, n, 2)
    nib = np.empty((g, 128, n, 4), np.uint8)
    nib[..., 0::2] = words & 0xF
    nib[..., 1::2] = words >> 4
    vals = E2M1[nib] * np.repeat(np.exp2(scales.astype(np.float64) - 127.0), 8, axis=1)[..., None]
    return vals.transpose(0, 1, 3, 2).reshape(g * 512, n)


def relu(v):
    return np.maximum(v, 0.0)


K, T, H, N = 1024, 1024, 512, 256


def setup_inputs():
    n = np.random.standard_normal
    s = mx_kscale(K)[:, None]
    u = mx_kscale(H)
    packed_xT = pack_fp4(n((K, T)) * s)
    return {
        "x_words": packed_xT[0],
        "x_scales": packed_xT[1],
        "w1": (n((K, H)) / np.sqrt(K) / s * u).astype(np.float32),
        "w2": (n((H, N)) / np.sqrt(2 * H) / u[:, None]).astype(np.float32),
        "w3": (n((H, N)) / np.sqrt(2 * H) / u[:, None]).astype(np.float32),
        "pos1": striped(np.random.permutation(T)),
        "pos2": striped(np.random.permutation(T)),
        "pos3": striped(np.random.permutation(T)),
        "pos4": striped(np.random.permutation(T)),
    }


def reference(x_words, x_scales, w1, w2, w3, pos1, pos2, pos3, pos4):
    xq = unpack_fp4(x_words, x_scales)
    h = relu(mxq(f64(w1), 0, "e4m3").T @ xq)
    z = (h[:, unstriped(pos1)] + h[:, unstriped(pos2)] + h[:, unstriped(pos3)] + h[:, unstriped(pos4)]) / 4
    return mxq(f64(w2), 0, "e4m3").T @ mxq(h, 0, "e4m3") + mxq(f64(w3), 0, "e4m3").T @ mxq(z, 0, "e4m3")

@@ -1,0 +1,305 @@
+from contextlib import ExitStack
+
+import concourse.mybir as mybir
+from concourse.masks import make_identity
+
+K, T, H, N = 1024, 1024, 512, 256
+FLOPS = 2 * K * H * T + 2 * 2 * H * N * T
+
+F32 = mybir.dt.float32
+BF16 = mybir.dt.bfloat16
+I32 = mybir.dt.int32
+U32 = mybir.dt.uint32
+U16 = mybir.dt.uint16
+U8 = mybir.dt.uint8
+FP8X4 = mybir.dt.float8_e4m3fn_x4
+FP4X4 = mybir.dt.float4_e2m1fn_x4
+ACT = mybir.ActivationFunctionType
+
+P = 128
+BANK = 512
+PASSES = K // 512
+CHUNKS = H // P
+LISTS = 4
+
+
+def tile_picked_wsagecat_mean_l_kernel(
+    tc, x_words, x_scales, w1, w2, w3, pos1, pos2, pos3, pos4, out
+):
+    nc = tc.nc
+    with ExitStack() as ctx:
+        keep = ctx.enter_context(tc.tile_pool(name="keep", bufs=1))
+        psum = ctx.enter_context(tc.psum_pool(name="psum", bufs=1))
+
+        def sbuf(name, shape, dtype):
+            return keep.tile(shape, dtype, name=name, align_bytes=64)
+
+        banks = [psum.tile([P, BANK], F32, name=f"bank{b}") for b in range(8)]
+        product_banks, sum_banks, turn_banks = banks[0:4], banks[4:6], banks[6:8]
+
+        ident = sbuf("ident", [P, P], F32)
+        make_identity(nc, ident[:])
+
+        xs = sbuf("xs", [P, PASSES, T], U8)
+        xs32 = xs[:].bitcast(I32)
+        nc.vector.memset(xs32, 0)
+        xs_src = x_scales.bitcast(I32).rearrange("z r c -> r z c")
+        for quad in range(4):
+            nc.scalar.dma_start(out=xs32[32 * quad : 32 * quad + 4], in_=xs_src[4 * quad : 4 * quad + 4])
+        warm = sbuf("warm", [P, 1], F32)
+        nc.scalar.activation(warm[:], ident[:, 0:1], ACT.Relu)
+
+        def load_w1(name, z, c0, c1):
+            raw = sbuf(name, [P, 4, (c1 - c0) * P], F32)
+            rows = w1[512 * z : 512 * (z + 1), c0 * P : c1 * P]
+            nc.sync.dma_start(out=raw[:], in_=rows.rearrange("(p j) c -> p j c", j=4))
+            return [raw[:, :, (c - c0) * P : (c - c0 + 1) * P] for c in range(c0, c1)]
+
+        w1_raw = {}
+        xw = []
+        for z in range(PASSES):
+            w1_raw[0, z] = load_w1(f"w1_first{z}", z, 0, 1)[0]
+            words = sbuf(f"xw{z}", [P, 2 * T], U8)
+            nc.sync.dma_start(out=words[:].bitcast(I32), in_=x_words[z].bitcast(I32))
+            xw.append(words)
+        lists = []
+        for d, pos in enumerate((pos1, pos2, pos3, pos4)):
+            offsets = keep.tile([P, T // 16], U16, name=f"list{d}")
+            nc.sync.dma_start(offsets[:], pos)
+            lists.append(offsets)
+        for z in range(PASSES):
+            w1_raw[1, z] = load_w1(f"w1_second{z}", z, 1, 2)[0]
+        for z in range(PASSES):
+            w1_raw[2, z], w1_raw[3, z] = load_w1(f"w1_rest{z}", z, 2, 4)
+        w23_raw = []
+        for s, w in enumerate((w2, w3)):
+            raw = sbuf(f"w23_raw{s}", [P, 4, N], F32)
+            nc.sync.dma_start(out=raw[:], in_=w.rearrange("(p j) n -> p j n", j=4))
+            w23_raw.append(raw)
+
+        w1_codes = [sbuf(f"w1_codes{c}", [P, PASSES * P], U32)[:] for c in range(2)]
+        w1_scales = [sbuf(f"w1_scales{c}", [P, PASSES * P], U8)[:] for c in range(2)]
+        rest_codes, rest_scales = sbuf("rest_codes", [P, 2 * PASSES * P], U32), sbuf("rest_scales", [P, 2 * PASSES * P], U8)
+        w1_codes = w1_codes + [rest_codes[:, 256 * r : 256 * (r + 1)] for r in range(2)]
+        w1_scales = w1_scales + [rest_scales[:, 256 * r : 256 * (r + 1)] for r in range(2)]
+        both_codes, both_scales = sbuf("both_codes", [P, 2 * N], U32), sbuf("both_scales", [P, 2 * N], U8)
+        w23_codes = [both_codes[:, N * s : N * (s + 1)] for s in range(2)]
+        w23_scales = [both_scales[:, N * s : N * (s + 1)] for s in range(2)]
+        h_codes, h_scales = sbuf("h_codes", [P, T], U32), sbuf("h_scales", [P, T], U8)
+        z_codes, z_scales = sbuf("z_codes", [P, T], U32), sbuf("z_scales", [P, T], U8)
+        h_rows = [sbuf(f"h_rows{c}", [P, T], F32) for c in range(CHUNKS)]
+        h_planes = sbuf("h_planes", [P, 4, T], F32)
+
+        def quantise(codes, scales, staged):
+            nc.vector.quantize_mx(out=codes.bitcast(FP8X4), scales=scales, in_=staged)
+
+        def round_w1(copy, c, z, staged):
+            copy(
+                staged.rearrange("p (u q e j) -> p q j u e", u=2, e=2, j=4),
+                w1_raw[c, z].rearrange("p j (q u e) -> p q j u e", u=2, e=2),
+            )
+
+        def interleave(staged, planes):
+            nc.scalar.copy(
+                staged.rearrange("p (c i t) -> p c t i", i=4, t=4),
+                planes.rearrange("p t (c i) -> p c t i", i=4),
+            )
+
+        def first_product_pass(c, z):
+            for half in range(2):
+                nc.tensor.matmul_mx(
+                    out=product_banks[2 * (c % 2) + half][:],
+                    lhsT=w1_codes[c][:, z * P : (z + 1) * P].bitcast(FP8X4),
+                    lhsT_scale=w1_scales[c][:, z * P : (z + 1) * P],
+                    rhs=xw[z][:, 2 * BANK * half : 2 * BANK * (half + 1)].bitcast(FP4X4),
+                    rhs_scale=xs[:, z, BANK * half : BANK * (half + 1)],
+                    start=(z == 0),
+                    stop=(z == PASSES - 1),
+                )
+
+        def relu_on_scalar(c, half):
+            nc.scalar.activation(
+                h_rows[c][:, BANK * half : BANK * (half + 1)], product_banks[2 * (c % 2) + half][:], ACT.Relu
+            )
+
+        def move_h(c):
+            for u in range(2):
+                for e in range(2):
+                    nc.sync.dma_start(
+                        out=h_planes[32 * c : 32 * (c + 1), 2 * u + e, :],
+                        in_=h_rows[c][64 * u + e : 64 * (u + 1) : 2, :],
+                    )
+
+        for z in range(PASSES):
+            staged = sbuf(f"w1_first_bf16_{z}", [P, 4 * P], BF16)
+            round_w1(nc.vector.tensor_copy, 0, z, staged[:])
+            quantise(w1_codes[0][:, z * P : (z + 1) * P], w1_scales[0][:, z * P : (z + 1) * P], staged[:])
+            first_product_pass(0, z)
+        relu_on_scalar(0, 0)
+        nc.vector.tensor_scalar_max(h_rows[0][:, BANK:], product_banks[1][:], 0.0)
+        move_h(0)
+
+        spans = [(0, 512), (512, 768), (768, 896), (896, 1024)]
+        steps = [(0, 0, 512), (0, 512, 1024), (1, 0, 512), (2, 0, 512), (3, 0, 512)]
+        steps = steps + [(c, v0, v1) for v0, v1 in spans[1:] for c in (1, 2, 3)]
+
+        rings = {
+            "first": ((0, 0), 512, 3),
+            "w1_second": ((0, 2), 512, 3),
+            "w1_rest": ((1, 0), 512, 3),
+            "w23": ((2, 2), 512, 3),
+            "h0": ((3, 3), 512, 3),
+            "h1": ((5, 0), 256, 5),
+            "z0": ((7, 2), 256, 5),
+            "z1": ((11, 0), 128, 5),
+            "z2": ((13, 1), 128, 3),
+        }
+        ring_tiles = {name: sbuf(f"ring_{name}", [P, width * slots], F32) for name, (key, width, slots) in rings.items()}
+        ring_at = {key: name for name, (key, width, slots) in rings.items()}
+        picked = {}
+        for n, (c, v0, v1) in enumerate(steps):
+            for d in range(LISTS):
+                if (n, d) in ring_at:
+                    name, turn = ring_at[n, d], 0
+                at = rings[name][1] * (turn % rings[name][2])
+                picked[n, d] = ring_tiles[name][:, at : at + v1 - v0]
+                turn = turn + 1
+
+        def staging(name):
+            key, width, slots = rings[name]
+            return ring_tiles[name][:, width // 2 : width * slots - width // 2]
+
+        second_staging = [ring_tiles["w1_second"][:, 384 + 512 * z : 640 + 512 * z].bitcast(BF16) for z in range(PASSES)]
+
+        z_turned = [sbuf(f"z_turned{s}", [P, (v1 - v0) // P, H], BF16) for s, (v0, v1) in enumerate(spans)]
+        z_last = sbuf("z_last", [P, 2 * P], F32)
+
+        def finish_chunk(c):
+            first_product_pass(c, PASSES - 1)
+            for half in range(2):
+                relu_on_scalar(c, half)
+            move_h(c)
+
+        def turn_back(s, b0, nb, words, bank):
+            turned = z_turned[s][:].bitcast(F32)
+            for b in range(nb):
+                for u in range(2):
+                    nc.tensor.transpose(
+                        bank[:, (2 * b + u) * P : (2 * b + u + 1) * P], turned[:, b0 + b, u * P : (u + 1) * P], ident[:]
+                    )
+            nc.scalar.copy(
+                words.rearrange("p (b v u) -> p b v u", b=nb, u=2),
+                bank[:, 0 : 2 * nb * P].rearrange("p (b u v) -> p b v u", b=nb, u=2),
+            )
+
+        def second_product(s, dests, reads):
+            v0, v1 = spans[s]
+            for m in range(N // P):
+                for side, (codes, scales) in enumerate(((h_codes, h_scales), (z_codes, z_scales))):
+                    nc.tensor.matmul_mx(
+                        out=dests[m],
+                        lhsT=w23_codes[side][:, m * P : (m + 1) * P].bitcast(FP8X4),
+                        lhsT_scale=w23_scales[side][:, m * P : (m + 1) * P],
+                        rhs=codes[:, v0:v1].bitcast(FP8X4),
+                        rhs_scale=scales[:, v0:v1],
+                        start=(side == 0),
+                        stop=(side == 1),
+                    )
+            result = sbuf(f"result{s}", [P, 2 * (v1 - v0)], F32)
+            at = 0
+            for read in reads:
+                nc.scalar.copy(result[:, at : at + read.shape[1]], read)
+                at = at + read.shape[1]
+            nc.sync.dma_start(
+                out=out[:, v0:v1].rearrange("(m p) v -> p m v", p=P),
+                in_=result[:].rearrange("p (m v) -> p m v", m=2),
+            )
+
+        def shared_bank_product(s, bank):
+            width = spans[s][1] - spans[s][0]
+            second_product(s, [bank[:, 0:width], bank[:, width : 2 * width]], [bank[:, 0 : 2 * width]])
+
+        for z in range(PASSES):
+            round_w1(nc.scalar.copy, 1, z, second_staging[z])
+        for c in (2, 3):
+            for z in range(PASSES):
+                at = 4 * P * (PASSES * (c - 2) + z)
+                round_w1(nc.scalar.copy, c, z, staging("w1_rest").bitcast(BF16)[:, at : at + 4 * P])
+
+        def quantise_second():
+            for z in range(PASSES):
+                quantise(w1_codes[1][:, z * P : (z + 1) * P], w1_scales[1][:, z * P : (z + 1) * P], second_staging[z])
+
+        def quantise_h(half):
+            cols = slice(BANK * half, BANK * (half + 1))
+            quantise(h_codes[:, cols], h_scales[:, cols], staging(f"h{half}").bitcast(BF16))
+
+        def finish_span(s, words):
+            v0, v1 = spans[s]
+            quantise(z_codes[:, v0:v1], z_scales[:, v0:v1], words.bitcast(BF16))
+            if s == 0:
+                second_product(0, [product_banks[0][:], product_banks[1][:]], [product_banks[0][:], product_banks[1][:]])
+            else:
+                shared_bank_product(s, product_banks[(s + 1) % 4])
+
+        before = {
+            rings["w1_second"][0]: [quantise_second, lambda: first_product_pass(1, 0)],
+            (0, 3): [lambda: finish_chunk(1)],
+            rings["w1_rest"][0]: [
+                lambda: quantise(rest_codes[:], rest_scales[:], staging("w1_rest").bitcast(BF16)),
+                lambda: first_product_pass(2, 0),
+            ],
+            (1, 1): [lambda: finish_chunk(2)],
+            (1, 2): [lambda: first_product_pass(3, 0)],
+            (1, 3): [lambda: finish_chunk(3)],
+            rings["w23"][0]: [lambda: quantise(both_codes[:], both_scales[:], staging("w23").bitcast(BF16))],
+            rings["h0"][0]: [lambda: quantise_h(0)],
+            rings["h1"][0]: [lambda: quantise_h(1)],
+            rings["z0"][0]: [lambda: finish_span(0, staging("z0"))],
+            rings["z1"][0]: [lambda: finish_span(1, staging("z1"))],
+            rings["z2"][0]: [lambda: finish_span(2, staging("z2"))],
+        }
+
+        for n, (c, v0, v1) in enumerate(steps):
+            bank = sum_banks[n % 2]
+            blocks = (v1 - v0) // P
+            for d in range(LISTS):
+                for work in before.get((n, d), []):
+                    work()
+                nc.vector.tensor_copy(picked[n, d], h_rows[c][:].indirect(lists[d][:, v0 // 16 : v1 // 16]))
+                for b in range(blocks):
+                    nc.tensor.matmul(
+                        bank[:, b * P : (b + 1) * P],
+                        picked[n, d][:, b * P : (b + 1) * P],
+                        ident[:],
+                        is_transpose=True,
+                        start=(d == 0 and b == 0),
+                        stop=(d == LISTS - 1 and b == blocks - 1),
+                    )
+            for s, (s0, s1) in enumerate(spans):
+                if v0 <= s0 and s1 <= v1:
+                    nc.scalar.activation(
+                        z_turned[s][:].rearrange("v b (u c r) -> v b u c r", u=2, c=CHUNKS)[:, :, :, c, :],
+                        bank[:, s0 - v0 : s1 - v0].rearrange("v (b u r) -> v b u r", u=2, r=64),
+                        ACT.Copy,
+                        scale=1.0 / LISTS,
+                    )
+            if n == 1:
+                for s in range(2):
+                    interleave(staging("w23").bitcast(BF16)[:, 4 * N * s : 4 * N * (s + 1)], w23_raw[s][:])
+            if n == 2:
+                for g in range(4):
+                    interleave(
+                        staging(f"h{g // 2}").bitcast(BF16)[:, 1024 * (g % 2) : 1024 * (g % 2 + 1)],
+                        h_planes[:, :, 256 * g : 256 * (g + 1)],
+                    )
+            if n == 4:
+                for g in range(2):
+                    turn_back(0, 2 * g, 2, staging("z0")[:, BANK * g : BANK * (g + 1)], turn_banks[g])
+            if n == 7:
+                turn_back(1, 0, 2, staging("z1"), turn_banks[0])
+            if n == 10:
+                turn_back(2, 0, 1, staging("z2"), turn_banks[1])
+            if n == 13:
+                turn_back(3, 0, 1, z_last[:], turn_banks[0])
+                finish_span(3, z_last[:])

@@ -37,17 +37,13 @@ def tile_picked_wsagecat_mean_l_kernel(
         banks = [psum.tile([P, BANK], F32, name=f"bank{b}") for b in range(8)]
         product_banks, sum_banks, turn_banks = banks[0:4], banks[4:6], banks[6:8]
 
-        ident = sbuf("ident", [P, P], F32)
-        make_identity(nc, ident[:])
-
         xs = sbuf("xs", [P, PASSES, T], U8)
         xs32 = xs[:].bitcast(I32)
-        nc.vector.memset(xs32, 0)
+        ident = sbuf("ident", [P, P], F32)
+        make_identity(nc, ident[:])
         xs_src = x_scales.bitcast(I32).rearrange("z r c -> r z c")
         for quad in range(4):
             nc.scalar.dma_start(out=xs32[32 * quad : 32 * quad + 4], in_=xs_src[4 * quad : 4 * quad + 4])
-        warm = sbuf("warm", [P, 1], F32)
-        nc.scalar.activation(warm[:], ident[:, 0:1], ACT.Relu)
 
         def load_w1(name, z, c0, c1):
             raw = sbuf(name, [P, 4, (c1 - c0) * P], F32)
@@ -62,13 +58,13 @@ def tile_picked_wsagecat_mean_l_kernel(
             words = sbuf(f"xw{z}", [P, 2 * T], U8)
             nc.sync.dma_start(out=words[:].bitcast(I32), in_=x_words[z].bitcast(I32))
             xw.append(words)
+        for z in range(PASSES):
+            w1_raw[1, z] = load_w1(f"w1_second{z}", z, 1, 2)[0]
         lists = []
         for d, pos in enumerate((pos1, pos2, pos3, pos4)):
             offsets = keep.tile([P, T // 16], U16, name=f"list{d}")
             nc.sync.dma_start(offsets[:], pos)
             lists.append(offsets)
-        for z in range(PASSES):
-            w1_raw[1, z] = load_w1(f"w1_second{z}", z, 1, 2)[0]
         for z in range(PASSES):
             w1_raw[2, z], w1_raw[3, z] = load_w1(f"w1_rest{z}", z, 2, 4)
         w23_raw = []
@@ -132,7 +128,11 @@ def tile_picked_wsagecat_mean_l_kernel(
 
         for z in range(PASSES):
             staged = sbuf(f"w1_first_bf16_{z}", [P, 4 * P], BF16)
-            round_w1(nc.vector.tensor_copy, 0, z, staged[:])
+            for u, copy in enumerate((nc.vector.tensor_copy, nc.scalar.copy)):
+                copy(
+                    staged[:].rearrange("p (u q e j) -> p u q j e", u=2, e=2, j=4)[:, u],
+                    w1_raw[0, z].rearrange("p j (q u e) -> p u q j e", u=2, e=2)[:, u],
+                )
             quantise(w1_codes[0][:, z * P : (z + 1) * P], w1_scales[0][:, z * P : (z + 1) * P], staged[:])
             first_product_pass(0, z)
         relu_on_scalar(0, 0)
@@ -141,18 +141,16 @@ def tile_picked_wsagecat_mean_l_kernel(
 
         spans = [(0, 512), (512, 768), (768, 896), (896, 1024)]
         steps = [(0, 0, 512), (0, 512, 1024), (1, 0, 512), (2, 0, 512), (3, 0, 512)]
-        steps = steps + [(c, v0, v1) for v0, v1 in spans[1:] for c in (1, 2, 3)]
+        steps = steps + [(1, 512, 1024), (2, 512, 768), (3, 512, 768), (2, 768, 1024), (3, 768, 896), (3, 896, 1024)]
 
         rings = {
             "first": ((0, 0), 512, 3),
             "w1_second": ((0, 2), 512, 3),
-            "w1_rest": ((1, 0), 512, 3),
-            "w23": ((2, 2), 512, 3),
-            "h0": ((3, 3), 512, 3),
-            "h1": ((5, 0), 256, 5),
-            "z0": ((7, 2), 256, 5),
-            "z1": ((11, 0), 128, 5),
-            "z2": ((13, 1), 128, 3),
+            "w1_rest": ((1, 1), 512, 4),
+            "h0": ((3, 3), 512, 4),
+            "h1": ((4, 3), 512, 4),
+            "z0": ((7, 0), 256, 5),
+            "z1": ((9, 2), 128, 5),
         }
         ring_tiles = {name: sbuf(f"ring_{name}", [P, width * slots], F32) for name, (key, width, slots) in rings.items()}
         ring_at = {key: name for name, (key, width, slots) in rings.items()}
@@ -167,12 +165,14 @@ def tile_picked_wsagecat_mean_l_kernel(
 
         def staging(name):
             key, width, slots = rings[name]
-            return ring_tiles[name][:, width // 2 : width * slots - width // 2]
+            return ring_tiles[name][:, width // 2 : width // 2 + (512 if name == "z1" else 1024)]
 
         second_staging = [ring_tiles["w1_second"][:, 384 + 512 * z : 640 + 512 * z].bitcast(BF16) for z in range(PASSES)]
 
         z_turned = [sbuf(f"z_turned{s}", [P, (v1 - v0) // P, H], BF16) for s, (v0, v1) in enumerate(spans)]
-        z_last = sbuf("z_last", [P, 2 * P], F32)
+        z_words = [staging("z0"), staging("z1")] + [sbuf(f"z_words{s}", [P, 2 * P], F32)[:] for s in (2, 3)]
+        w23_bf16 = sbuf("w23_bf16", [P, 2 * 4 * N], BF16)
+        h_bf16 = [staging(f"h{half}").bitcast(BF16) for half in range(2)]
 
         def finish_chunk(c):
             first_product_pass(c, PASSES - 1)
@@ -205,6 +205,12 @@ def tile_picked_wsagecat_mean_l_kernel(
                         start=(side == 0),
                         stop=(side == 1),
                     )
+            if s == 3:
+                for m, (copy, queue) in enumerate(((nc.scalar.copy, nc.scalar), (nc.vector.tensor_copy, nc.sync))):
+                    result = sbuf(f"result{s}_{m}", [P, v1 - v0], F32)
+                    copy(result[:], reads[m])
+                    queue.dma_start(out=out[m * P : (m + 1) * P, v0:v1], in_=result[:])
+                return
             result = sbuf(f"result{s}", [P, 2 * (v1 - v0)], F32)
             at = 0
             for read in reads:
@@ -232,13 +238,14 @@ def tile_picked_wsagecat_mean_l_kernel(
 
         def quantise_h(half):
             cols = slice(BANK * half, BANK * (half + 1))
-            quantise(h_codes[:, cols], h_scales[:, cols], staging(f"h{half}").bitcast(BF16))
+            quantise(h_codes[:, cols], h_scales[:, cols], h_bf16[half])
 
-        def finish_span(s, words):
+        def finish_span(s):
             v0, v1 = spans[s]
-            quantise(z_codes[:, v0:v1], z_scales[:, v0:v1], words.bitcast(BF16))
-            if s == 0:
-                second_product(0, [product_banks[0][:], product_banks[1][:]], [product_banks[0][:], product_banks[1][:]])
+            quantise(z_codes[:, v0:v1], z_scales[:, v0:v1], z_words[s].bitcast(BF16))
+            if s in (0, 3):
+                width = v1 - v0
+                second_product(s, [bank[:, 0:width] for bank in product_banks[0:2]], [bank[:, 0:width] for bank in product_banks[0:2]])
             else:
                 shared_bank_product(s, product_banks[(s + 1) % 4])
 
@@ -249,15 +256,13 @@ def tile_picked_wsagecat_mean_l_kernel(
                 lambda: quantise(rest_codes[:], rest_scales[:], staging("w1_rest").bitcast(BF16)),
                 lambda: first_product_pass(2, 0),
             ],
-            (1, 1): [lambda: finish_chunk(2)],
-            (1, 2): [lambda: first_product_pass(3, 0)],
-            (1, 3): [lambda: finish_chunk(3)],
-            rings["w23"][0]: [lambda: quantise(both_codes[:], both_scales[:], staging("w23").bitcast(BF16))],
+            (1, 2): [lambda: finish_chunk(2)],
+            (1, 3): [lambda: first_product_pass(3, 0)],
+            (2, 0): [lambda: finish_chunk(3)],
             rings["h0"][0]: [lambda: quantise_h(0)],
             rings["h1"][0]: [lambda: quantise_h(1)],
-            rings["z0"][0]: [lambda: finish_span(0, staging("z0"))],
-            rings["z1"][0]: [lambda: finish_span(1, staging("z1"))],
-            rings["z2"][0]: [lambda: finish_span(2, staging("z2"))],
+            rings["z0"][0]: [lambda: finish_span(0)],
+            rings["z1"][0]: [lambda: finish_span(1)],
         }
 
         for n, (c, v0, v1) in enumerate(steps):
@@ -286,20 +291,21 @@ def tile_picked_wsagecat_mean_l_kernel(
                     )
             if n == 1:
                 for s in range(2):
-                    interleave(staging("w23").bitcast(BF16)[:, 4 * N * s : 4 * N * (s + 1)], w23_raw[s][:])
+                    interleave(w23_bf16[:, 4 * N * s : 4 * N * (s + 1)], w23_raw[s][:])
+                quantise(both_codes[:], both_scales[:], w23_bf16[:])
             if n == 2:
-                for g in range(4):
-                    interleave(
-                        staging(f"h{g // 2}").bitcast(BF16)[:, 1024 * (g % 2) : 1024 * (g % 2 + 1)],
-                        h_planes[:, :, 256 * g : 256 * (g + 1)],
-                    )
+                for half in range(2):
+                    for g in range(2):
+                        v = BANK * half + 256 * g
+                        interleave(h_bf16[half][:, 1024 * g : 1024 * (g + 1)], h_planes[:, :, v : v + 256])
             if n == 4:
                 for g in range(2):
-                    turn_back(0, 2 * g, 2, staging("z0")[:, BANK * g : BANK * (g + 1)], turn_banks[g])
+                    turn_back(0, 2 * g, 2, z_words[0][:, BANK * g : BANK * (g + 1)], turn_banks[g])
             if n == 7:
-                turn_back(1, 0, 2, staging("z1"), turn_banks[0])
+                turn_back(1, 0, 2, z_words[1], turn_banks[0])
+            if n == 9:
+                turn_back(2, 0, 1, z_words[2], turn_banks[1])
+                finish_span(2)
             if n == 10:
-                turn_back(2, 0, 1, staging("z2"), turn_banks[1])
-            if n == 13:
-                turn_back(3, 0, 1, z_last[:], turn_banks[0])
-                finish_span(3, z_last[:])
+                turn_back(3, 0, 1, z_words[3], turn_banks[0])
+                finish_span(3)

@@ -89,17 +89,8 @@ def tile_picked_wsagecat_mean_l_kernel(
         def quantise(codes, scales, staged):
             nc.vector.quantize_mx(out=codes.bitcast(FP8X4), scales=scales, in_=staged)
 
-        def round_w1(copy, c, z, staged):
-            copy(
-                staged.rearrange("p (u q e j) -> p q j u e", u=2, e=2, j=4),
-                w1_raw[c, z].rearrange("p j (q u e) -> p q j u e", u=2, e=2),
-            )
-
-        def interleave(staged, planes):
-            nc.scalar.copy(
-                staged.rearrange("p (c i t) -> p c t i", i=4, t=4),
-                planes.rearrange("p t (c i) -> p c t i", i=4),
-            )
+        def interleave(staged, planes, copy=nc.scalar.copy):
+            copy(staged.rearrange("p (c t) -> p c t", t=4), planes.rearrange("p t c -> p c t"))
 
         def first_product_pass(c, z):
             for half in range(2):
@@ -119,20 +110,13 @@ def tile_picked_wsagecat_mean_l_kernel(
             )
 
         def move_h(c):
-            for u in range(2):
-                for e in range(2):
-                    nc.sync.dma_start(
-                        out=h_planes[32 * c : 32 * (c + 1), 2 * u + e, :],
-                        in_=h_rows[c][64 * u + e : 64 * (u + 1) : 2, :],
-                    )
+            for t in range(4):
+                nc.sync.dma_start(out=h_planes[32 * c : 32 * (c + 1), t, :], in_=h_rows[c][t:P:4, :])
 
         for z in range(PASSES):
             staged = sbuf(f"w1_first_bf16_{z}", [P, 4 * P], BF16)
-            for u, copy in enumerate((nc.vector.tensor_copy, nc.scalar.copy)):
-                copy(
-                    staged[:].rearrange("p (u q e j) -> p u q j e", u=2, e=2, j=4)[:, u],
-                    w1_raw[0, z].rearrange("p j (q u e) -> p u q j e", u=2, e=2)[:, u],
-                )
+            interleave(staged[:, 0 : 4 * 88], w1_raw[0, z][:, :, 0:88], nc.vector.tensor_copy)
+            interleave(staged[:, 4 * 88 :], w1_raw[0, z][:, :, 88:])
             quantise(w1_codes[0][:, z * P : (z + 1) * P], w1_scales[0][:, z * P : (z + 1) * P], staged[:])
             first_product_pass(0, z)
         relu_on_scalar(0, 0)
@@ -226,11 +210,11 @@ def tile_picked_wsagecat_mean_l_kernel(
             second_product(s, [bank[:, 0:width], bank[:, width : 2 * width]], [bank[:, 0 : 2 * width]])
 
         for z in range(PASSES):
-            round_w1(nc.scalar.copy, 1, z, second_staging[z])
+            interleave(second_staging[z], w1_raw[1, z])
         for c in (2, 3):
             for z in range(PASSES):
                 at = 4 * P * (PASSES * (c - 2) + z)
-                round_w1(nc.scalar.copy, c, z, staging("w1_rest").bitcast(BF16)[:, at : at + 4 * P])
+                interleave(staging("w1_rest").bitcast(BF16)[:, at : at + 4 * P], w1_raw[c, z])
 
         def quantise_second():
             for z in range(PASSES):
@@ -283,12 +267,13 @@ def tile_picked_wsagecat_mean_l_kernel(
                     )
             for s, (s0, s1) in enumerate(spans):
                 if v0 <= s0 and s1 <= v1:
-                    nc.scalar.activation(
-                        z_turned[s][:].rearrange("v b (u c r) -> v b u c r", u=2, c=CHUNKS)[:, :, :, c, :],
-                        bank[:, s0 - v0 : s1 - v0].rearrange("v (b u r) -> v b u r", u=2, r=64),
-                        ACT.Copy,
-                        scale=1.0 / LISTS,
-                    )
+                    dest = z_turned[s][:].rearrange("v b (u c q e) -> v c u b q e", u=2, c=CHUNKS, e=2)[:, c]
+                    sums = bank[:, s0 - v0 : s1 - v0].rearrange("v (b q u e) -> v u b q e", q=32, u=2, e=2)
+                    if s1 - s0 == P:
+                        nc.scalar.activation(dest[:, :, 0], sums[:, :, 0], ACT.Copy, scale=1.0 / LISTS)
+                    else:
+                        for u in range(2):
+                            nc.scalar.activation(dest[:, u], sums[:, u], ACT.Copy, scale=1.0 / LISTS)
             if n == 1:
                 for s in range(2):
                     interleave(w23_bf16[:, 4 * N * s : 4 * N * (s + 1)], w23_raw[s][:])

@@ -129,10 +129,9 @@ def tile_picked_wsagecat_mean_l_kernel(
 
         rings = {
             "first": ((0, 0), 512, 3),
-            "w1_second": ((0, 2), 512, 3),
-            "w1_rest": ((1, 1), 512, 4),
-            "h0": ((3, 3), 512, 4),
-            "h1": ((4, 3), 512, 4),
+            "w1_second": ((0, 3), 512, 3),
+            "w1_rest": ((1, 2), 512, 4),
+            "h0": ((4, 3), 512, 4),
             "z0": ((7, 0), 256, 5),
             "z1": ((9, 2), 128, 5),
         }
@@ -149,14 +148,18 @@ def tile_picked_wsagecat_mean_l_kernel(
 
         def staging(name):
             key, width, slots = rings[name]
-            return ring_tiles[name][:, width // 2 : width // 2 + (512 if name == "z1" else 1024)]
+            return ring_tiles[name][:, width // 2 : width // 2 + (512 if name in ("h0", "z1") else 1024)]
 
         second_staging = [ring_tiles["w1_second"][:, 384 + 512 * z : 640 + 512 * z].bitcast(BF16) for z in range(PASSES)]
 
         z_turned = [sbuf(f"z_turned{s}", [P, (v1 - v0) // P, H], BF16) for s, (v0, v1) in enumerate(spans)]
         z_words = [staging("z0"), staging("z1")] + [sbuf(f"z_words{s}", [P, 2 * P], F32)[:] for s in (2, 3)]
         w23_bf16 = sbuf("w23_bf16", [P, 2 * 4 * N], BF16)
-        h_bf16 = [staging(f"h{half}").bitcast(BF16) for half in range(2)]
+        h_bf16 = {
+            (0, 256): staging("h0").bitcast(BF16),
+            (256, 512): sbuf("h_bf16_a", [P, 4 * 256], BF16)[:],
+            (512, 1024): sbuf("h_bf16_b", [P, 4 * 512], BF16)[:],
+        }
 
         def finish_chunk(c):
             first_product_pass(c, PASSES - 1)
@@ -176,12 +179,14 @@ def tile_picked_wsagecat_mean_l_kernel(
                 bank[:, 0 : 2 * nb * P].rearrange("p (b u v) -> p b v u", b=nb, u=2),
             )
 
-        def second_product(s, dests, reads):
+        def second_product(s):
             v0, v1 = spans[s]
+            last = s == len(spans) - 1
             for m in range(N // P):
+                sums = product_banks[2 * (s % 2) + m][:, 0 : v1 - v0]
                 for side, (codes, scales) in enumerate(((h_codes, h_scales), (z_codes, z_scales))):
                     nc.tensor.matmul_mx(
-                        out=dests[m],
+                        out=sums,
                         lhsT=w23_codes[side][:, m * P : (m + 1) * P].bitcast(FP8X4),
                         lhsT_scale=w23_scales[side][:, m * P : (m + 1) * P],
                         rhs=codes[:, v0:v1].bitcast(FP8X4),
@@ -189,25 +194,11 @@ def tile_picked_wsagecat_mean_l_kernel(
                         start=(side == 0),
                         stop=(side == 1),
                     )
-            if s == 3:
-                for m, (copy, queue) in enumerate(((nc.scalar.copy, nc.scalar), (nc.vector.tensor_copy, nc.sync))):
-                    result = sbuf(f"result{s}_{m}", [P, v1 - v0], F32)
-                    copy(result[:], reads[m])
-                    queue.dma_start(out=out[m * P : (m + 1) * P, v0:v1], in_=result[:])
-                return
-            result = sbuf(f"result{s}", [P, 2 * (v1 - v0)], F32)
-            at = 0
-            for read in reads:
-                nc.scalar.copy(result[:, at : at + read.shape[1]], read)
-                at = at + read.shape[1]
-            nc.sync.dma_start(
-                out=out[:, v0:v1].rearrange("(m p) v -> p m v", p=P),
-                in_=result[:].rearrange("p (m v) -> p m v", m=2),
-            )
-
-        def shared_bank_product(s, bank):
-            width = spans[s][1] - spans[s][0]
-            second_product(s, [bank[:, 0:width], bank[:, width : 2 * width]], [bank[:, 0 : 2 * width]])
+                result = sbuf(f"result{s}_{m}", [P, v1 - v0], F32)
+                copy = nc.vector.tensor_copy if last and m == 1 else nc.scalar.copy
+                queue = nc.scalar if last and m == 0 else nc.sync
+                copy(result[:], sums)
+                queue.dma_start(out=out[m * P : (m + 1) * P, v0:v1], in_=result[:])
 
         for z in range(PASSES):
             interleave(second_staging[z], w1_raw[1, z])
@@ -220,31 +211,25 @@ def tile_picked_wsagecat_mean_l_kernel(
             for z in range(PASSES):
                 quantise(w1_codes[1][:, z * P : (z + 1) * P], w1_scales[1][:, z * P : (z + 1) * P], second_staging[z])
 
-        def quantise_h(half):
-            cols = slice(BANK * half, BANK * (half + 1))
-            quantise(h_codes[:, cols], h_scales[:, cols], h_bf16[half])
+        def quantise_h(v0, v1):
+            quantise(h_codes[:, v0:v1], h_scales[:, v0:v1], h_bf16[v0, v1])
 
         def finish_span(s):
             v0, v1 = spans[s]
             quantise(z_codes[:, v0:v1], z_scales[:, v0:v1], z_words[s].bitcast(BF16))
-            if s in (0, 3):
-                width = v1 - v0
-                second_product(s, [bank[:, 0:width] for bank in product_banks[0:2]], [bank[:, 0:width] for bank in product_banks[0:2]])
-            else:
-                shared_bank_product(s, product_banks[(s + 1) % 4])
+            second_product(s)
 
         before = {
             rings["w1_second"][0]: [quantise_second, lambda: first_product_pass(1, 0)],
-            (0, 3): [lambda: finish_chunk(1)],
+            (1, 0): [lambda: finish_chunk(1)],
             rings["w1_rest"][0]: [
                 lambda: quantise(rest_codes[:], rest_scales[:], staging("w1_rest").bitcast(BF16)),
                 lambda: first_product_pass(2, 0),
             ],
-            (1, 2): [lambda: finish_chunk(2)],
-            (1, 3): [lambda: first_product_pass(3, 0)],
-            (2, 0): [lambda: finish_chunk(3)],
-            rings["h0"][0]: [lambda: quantise_h(0)],
-            rings["h1"][0]: [lambda: quantise_h(1)],
+            (1, 3): [lambda: finish_chunk(2)],
+            (2, 0): [lambda: first_product_pass(3, 0)],
+            (2, 1): [lambda: finish_chunk(3)],
+            rings["h0"][0]: [lambda: quantise_h(0, 256)],
             rings["z0"][0]: [lambda: finish_span(0)],
             rings["z1"][0]: [lambda: finish_span(1)],
         }
@@ -279,10 +264,11 @@ def tile_picked_wsagecat_mean_l_kernel(
                     interleave(w23_bf16[:, 4 * N * s : 4 * N * (s + 1)], w23_raw[s][:])
                 quantise(both_codes[:], both_scales[:], w23_bf16[:])
             if n == 2:
-                for half in range(2):
-                    for g in range(2):
-                        v = BANK * half + 256 * g
-                        interleave(h_bf16[half][:, 1024 * g : 1024 * (g + 1)], h_planes[:, :, v : v + 256])
+                for h0, h1 in h_bf16:
+                    for v in range(h0, h1, 256):
+                        interleave(h_bf16[h0, h1][:, 4 * (v - h0) : 4 * (v - h0 + 256)], h_planes[:, :, v : v + 256])
+                    if h0 > 0:
+                        quantise_h(h0, h1)
             if n == 4:
                 for g in range(2):
                     turn_back(0, 2 * g, 2, z_words[0][:, BANK * g : BANK * (g + 1)], turn_banks[g])

from contextlib import ExitStack

import concourse.mybir as mybir
from concourse.masks import make_identity

K, T, H, N = 1024, 1024, 512, 256
FLOPS = 2 * K * H * T + 2 * 2 * H * N * T

F32 = mybir.dt.float32
BF16 = mybir.dt.bfloat16
I32 = mybir.dt.int32
U32 = mybir.dt.uint32
U16 = mybir.dt.uint16
U8 = mybir.dt.uint8
FP8X4 = mybir.dt.float8_e4m3fn_x4
FP4X4 = mybir.dt.float4_e2m1fn_x4
ACT = mybir.ActivationFunctionType

P = 128
BANK = 512
PASSES = K // 512
CHUNKS = H // P
LISTS = 4


def tile_picked_wsagecat_mean_l_kernel(
    tc, x_words, x_scales, w1, w2, w3, pos1, pos2, pos3, pos4, out
):
    nc = tc.nc
    with ExitStack() as ctx:
        keep = ctx.enter_context(tc.tile_pool(name="keep", bufs=1))
        psum = ctx.enter_context(tc.psum_pool(name="psum", bufs=1))

        def sbuf(name, shape, dtype):
            return keep.tile(shape, dtype, name=name, align_bytes=64)

        banks = [psum.tile([P, BANK], F32, name=f"bank{b}") for b in range(8)]
        product_banks, sum_banks, turn_banks = banks[0:4], banks[4:6], banks[6:8]

        xs = sbuf("xs", [P, PASSES, T], U8)
        xs32 = xs[:].bitcast(I32)
        ident = sbuf("ident", [P, P], F32)
        make_identity(nc, ident[:])
        xs_src = x_scales.bitcast(I32).rearrange("z r c -> r z c")
        for quad in range(4):
            nc.scalar.dma_start(out=xs32[32 * quad : 32 * quad + 4], in_=xs_src[4 * quad : 4 * quad + 4])

        def load_w1(name, z, c0, c1):
            raw = sbuf(name, [P, 4, (c1 - c0) * P], F32)
            rows = w1[512 * z : 512 * (z + 1), c0 * P : c1 * P]
            nc.sync.dma_start(out=raw[:], in_=rows.rearrange("(p j) c -> p j c", j=4))
            return [raw[:, :, (c - c0) * P : (c - c0 + 1) * P] for c in range(c0, c1)]

        w1_raw = {}
        xw = []
        for z in range(PASSES):
            w1_raw[0, z] = load_w1(f"w1_first{z}", z, 0, 1)[0]
            words = sbuf(f"xw{z}", [P, 2 * T], U8)
            nc.sync.dma_start(out=words[:].bitcast(I32), in_=x_words[z].bitcast(I32))
            xw.append(words)
        for z in range(PASSES):
            w1_raw[1, z] = load_w1(f"w1_second{z}", z, 1, 2)[0]
        lists = []
        for d, pos in enumerate((pos1, pos2, pos3, pos4)):
            offsets = keep.tile([P, T // 16], U16, name=f"list{d}")
            nc.sync.dma_start(offsets[:], pos)
            lists.append(offsets)
        for z in range(PASSES):
            w1_raw[2, z], w1_raw[3, z] = load_w1(f"w1_rest{z}", z, 2, 4)
        w23_raw = []
        for s, w in enumerate((w2, w3)):
            raw = sbuf(f"w23_raw{s}", [P, 4, N], F32)
            nc.sync.dma_start(out=raw[:], in_=w.rearrange("(p j) n -> p j n", j=4))
            w23_raw.append(raw)

        w1_codes = [sbuf(f"w1_codes{c}", [P, PASSES * P], U32)[:] for c in range(2)]
        w1_scales = [sbuf(f"w1_scales{c}", [P, PASSES * P], U8)[:] for c in range(2)]
        rest_codes, rest_scales = sbuf("rest_codes", [P, 2 * PASSES * P], U32), sbuf("rest_scales", [P, 2 * PASSES * P], U8)
        w1_codes = w1_codes + [rest_codes[:, 256 * r : 256 * (r + 1)] for r in range(2)]
        w1_scales = w1_scales + [rest_scales[:, 256 * r : 256 * (r + 1)] for r in range(2)]
        both_codes, both_scales = sbuf("both_codes", [P, 2 * N], U32), sbuf("both_scales", [P, 2 * N], U8)
        w23_codes = [both_codes[:, N * s : N * (s + 1)] for s in range(2)]
        w23_scales = [both_scales[:, N * s : N * (s + 1)] for s in range(2)]
        h_codes, h_scales = sbuf("h_codes", [P, T], U32), sbuf("h_scales", [P, T], U8)
        z_codes, z_scales = sbuf("z_codes", [P, T], U32), sbuf("z_scales", [P, T], U8)
        h_rows = [sbuf(f"h_rows{c}", [P, T], F32) for c in range(CHUNKS)]
        h_planes = sbuf("h_planes", [P, 4, T], F32)

        def quantise(codes, scales, staged):
            nc.vector.quantize_mx(out=codes.bitcast(FP8X4), scales=scales, in_=staged)

        def interleave(staged, planes, copy=nc.scalar.copy):
            copy(staged.rearrange("p (c t) -> p c t", t=4), planes.rearrange("p t c -> p c t"))

        def first_product_pass(c, z):
            for half in range(2):
                nc.tensor.matmul_mx(
                    out=product_banks[2 * (c % 2) + half][:],
                    lhsT=w1_codes[c][:, z * P : (z + 1) * P].bitcast(FP8X4),
                    lhsT_scale=w1_scales[c][:, z * P : (z + 1) * P],
                    rhs=xw[z][:, 2 * BANK * half : 2 * BANK * (half + 1)].bitcast(FP4X4),
                    rhs_scale=xs[:, z, BANK * half : BANK * (half + 1)],
                    start=(z == 0),
                    stop=(z == PASSES - 1),
                )

        def relu_on_scalar(c, half):
            nc.scalar.activation(
                h_rows[c][:, BANK * half : BANK * (half + 1)], product_banks[2 * (c % 2) + half][:], ACT.Relu
            )

        def move_h(c):
            for t in range(4):
                nc.sync.dma_start(out=h_planes[32 * c : 32 * (c + 1), t, :], in_=h_rows[c][t:P:4, :])

        for z in range(PASSES):
            staged = sbuf(f"w1_first_bf16_{z}", [P, 4 * P], BF16)
            interleave(staged[:, 0 : 4 * 88], w1_raw[0, z][:, :, 0:88], nc.vector.tensor_copy)
            interleave(staged[:, 4 * 88 :], w1_raw[0, z][:, :, 88:])
            quantise(w1_codes[0][:, z * P : (z + 1) * P], w1_scales[0][:, z * P : (z + 1) * P], staged[:])
            first_product_pass(0, z)
        relu_on_scalar(0, 0)
        nc.vector.tensor_scalar_max(h_rows[0][:, BANK:], product_banks[1][:], 0.0)
        move_h(0)

        spans = [(0, 512), (512, 768), (768, 896), (896, 1024)]
        steps = [(0, 0, 512), (0, 512, 1024), (1, 0, 512), (2, 0, 512), (3, 0, 512)]
        steps = steps + [(1, 512, 1024), (2, 512, 768), (3, 512, 768), (2, 768, 1024), (3, 768, 896), (3, 896, 1024)]

        rings = {
            "first": ((0, 0), 512, 3),
            "w1_second": ((0, 3), 512, 3),
            "w1_rest": ((1, 2), 512, 4),
            "h0": ((4, 3), 512, 4),
            "z0": ((7, 0), 256, 5),
            "z1": ((9, 2), 128, 5),
        }
        ring_tiles = {name: sbuf(f"ring_{name}", [P, width * slots], F32) for name, (key, width, slots) in rings.items()}
        ring_at = {key: name for name, (key, width, slots) in rings.items()}
        picked = {}
        for n, (c, v0, v1) in enumerate(steps):
            for d in range(LISTS):
                if (n, d) in ring_at:
                    name, turn = ring_at[n, d], 0
                at = rings[name][1] * (turn % rings[name][2])
                picked[n, d] = ring_tiles[name][:, at : at + v1 - v0]
                turn = turn + 1

        def staging(name):
            key, width, slots = rings[name]
            return ring_tiles[name][:, width // 2 : width // 2 + (512 if name in ("h0", "z1") else 1024)]

        second_staging = [ring_tiles["w1_second"][:, 384 + 512 * z : 640 + 512 * z].bitcast(BF16) for z in range(PASSES)]

        z_turned = [sbuf(f"z_turned{s}", [P, (v1 - v0) // P, H], BF16) for s, (v0, v1) in enumerate(spans)]
        z_words = [staging("z0"), staging("z1")] + [sbuf(f"z_words{s}", [P, 2 * P], F32)[:] for s in (2, 3)]
        w23_bf16 = sbuf("w23_bf16", [P, 2 * 4 * N], BF16)
        h_bf16 = {
            (0, 256): staging("h0").bitcast(BF16),
            (256, 512): sbuf("h_bf16_a", [P, 4 * 256], BF16)[:],
            (512, 1024): sbuf("h_bf16_b", [P, 4 * 512], BF16)[:],
        }

        def finish_chunk(c):
            first_product_pass(c, PASSES - 1)
            for half in range(2):
                relu_on_scalar(c, half)
            move_h(c)

        def turn_back(s, b0, nb, words, bank):
            turned = z_turned[s][:].bitcast(F32)
            for b in range(nb):
                for u in range(2):
                    nc.tensor.transpose(
                        bank[:, (2 * b + u) * P : (2 * b + u + 1) * P], turned[:, b0 + b, u * P : (u + 1) * P], ident[:]
                    )
            nc.scalar.copy(
                words.rearrange("p (b v u) -> p b v u", b=nb, u=2),
                bank[:, 0 : 2 * nb * P].rearrange("p (b u v) -> p b v u", b=nb, u=2),
            )

        def second_product(s):
            v0, v1 = spans[s]
            last = s == len(spans) - 1
            for m in range(N // P):
                sums = product_banks[2 * (s % 2) + m][:, 0 : v1 - v0]
                for side, (codes, scales) in enumerate(((h_codes, h_scales), (z_codes, z_scales))):
                    nc.tensor.matmul_mx(
                        out=sums,
                        lhsT=w23_codes[side][:, m * P : (m + 1) * P].bitcast(FP8X4),
                        lhsT_scale=w23_scales[side][:, m * P : (m + 1) * P],
                        rhs=codes[:, v0:v1].bitcast(FP8X4),
                        rhs_scale=scales[:, v0:v1],
                        start=(side == 0),
                        stop=(side == 1),
                    )
                result = sbuf(f"result{s}_{m}", [P, v1 - v0], F32)
                copy = nc.vector.tensor_copy if last and m == 1 else nc.scalar.copy
                queue = nc.scalar if last and m == 0 else nc.sync
                copy(result[:], sums)
                queue.dma_start(out=out[m * P : (m + 1) * P, v0:v1], in_=result[:])

        for z in range(PASSES):
            interleave(second_staging[z], w1_raw[1, z])
        for c in (2, 3):
            for z in range(PASSES):
                at = 4 * P * (PASSES * (c - 2) + z)
                interleave(staging("w1_rest").bitcast(BF16)[:, at : at + 4 * P], w1_raw[c, z])

        def quantise_second():
            for z in range(PASSES):
                quantise(w1_codes[1][:, z * P : (z + 1) * P], w1_scales[1][:, z * P : (z + 1) * P], second_staging[z])

        def quantise_h(v0, v1):
            quantise(h_codes[:, v0:v1], h_scales[:, v0:v1], h_bf16[v0, v1])

        def finish_span(s):
            v0, v1 = spans[s]
            quantise(z_codes[:, v0:v1], z_scales[:, v0:v1], z_words[s].bitcast(BF16))
            second_product(s)

        before = {
            rings["w1_second"][0]: [quantise_second, lambda: first_product_pass(1, 0)],
            (1, 0): [lambda: finish_chunk(1)],
            rings["w1_rest"][0]: [
                lambda: quantise(rest_codes[:], rest_scales[:], staging("w1_rest").bitcast(BF16)),
                lambda: first_product_pass(2, 0),
            ],
            (1, 3): [lambda: finish_chunk(2)],
            (2, 0): [lambda: first_product_pass(3, 0)],
            (2, 1): [lambda: finish_chunk(3)],
            rings["h0"][0]: [lambda: quantise_h(0, 256)],
            rings["z0"][0]: [lambda: finish_span(0)],
            rings["z1"][0]: [lambda: finish_span(1)],
        }

        for n, (c, v0, v1) in enumerate(steps):
            bank = sum_banks[n % 2]
            blocks = (v1 - v0) // P
            for d in range(LISTS):
                for work in before.get((n, d), []):
                    work()
                nc.vector.tensor_copy(picked[n, d], h_rows[c][:].indirect(lists[d][:, v0 // 16 : v1 // 16]))
                for b in range(blocks):
                    nc.tensor.matmul(
                        bank[:, b * P : (b + 1) * P],
                        picked[n, d][:, b * P : (b + 1) * P],
                        ident[:],
                        is_transpose=True,
                        start=(d == 0 and b == 0),
                        stop=(d == LISTS - 1 and b == blocks - 1),
                    )
            for s, (s0, s1) in enumerate(spans):
                if v0 <= s0 and s1 <= v1:
                    dest = z_turned[s][:].rearrange("v b (u c q e) -> v c u b q e", u=2, c=CHUNKS, e=2)[:, c]
                    sums = bank[:, s0 - v0 : s1 - v0].rearrange("v (b q u e) -> v u b q e", q=32, u=2, e=2)
                    if s1 - s0 == P:
                        nc.scalar.activation(dest[:, :, 0], sums[:, :, 0], ACT.Copy, scale=1.0 / LISTS)
                    else:
                        for u in range(2):
                            nc.scalar.activation(dest[:, u], sums[:, u], ACT.Copy, scale=1.0 / LISTS)
            if n == 1:
                for s in range(2):
                    interleave(w23_bf16[:, 4 * N * s : 4 * N * (s + 1)], w23_raw[s][:])
                quantise(both_codes[:], both_scales[:], w23_bf16[:])
            if n == 2:
                for h0, h1 in h_bf16:
                    for v in range(h0, h1, 256):
                        interleave(h_bf16[h0, h1][:, 4 * (v - h0) : 4 * (v - h0 + 256)], h_planes[:, :, v : v + 256])
                    if h0 > 0:
                        quantise_h(h0, h1)
            if n == 4:
                for g in range(2):
                    turn_back(0, 2 * g, 2, z_words[0][:, BANK * g : BANK * (g + 1)], turn_banks[g])
            if n == 7:
                turn_back(1, 0, 2, z_words[1], turn_banks[0])
            if n == 9:
                turn_back(2, 0, 1, z_words[2], turn_banks[1])
                finish_span(2)
            if n == 10:
                turn_back(3, 0, 1, z_words[3], turn_banks[0])
                finish_span(3)
